import numpy as np
import ml_dtypes


def mxq(x, axis, fmt="e4m3"):
    dtype, down = {"e4m3": (ml_dtypes.float8_e4m3fn, 7), "e5m2": (ml_dtypes.float8_e5m2, 14)}[fmt]
    v = np.moveaxis(np.asarray(x, np.float32).astype(ml_dtypes.bfloat16).astype(np.float64), axis, -1)
    blocks = v.reshape(v.shape[:-1] + (-1, 32))
    amax = np.abs(blocks).max(-1, keepdims=True)
    byte = np.maximum(np.where(amax > 0, np.frexp(amax)[1] - 1 + 127, 0) - down, 1)
    scale = np.exp2(byte - 127.0)
    codes = (blocks / scale).astype(np.float32).astype(dtype).astype(np.float64)
    return np.moveaxis((codes * scale).reshape(v.shape), -1, axis)


WIDE = False


def mx_kscale(k):
    if not WIDE:
        return np.ones(k)
    levels = np.array([10, -10, 5, -5, 0])
    if k % 512:
        return np.exp2(np.random.permutation(np.resize(levels, k // 32))).repeat(32)
    a = np.empty((k // 512, 16))
    for p in range(k // 512):
        a[p, :8] = np.random.permutation(np.resize(levels, 8))
        for g in range(8):
            far = levels[np.abs(levels - a[p, g]) >= 10]
            a[p, g + 8] = far[np.random.randint(len(far))]
    return np.exp2(a.ravel()).repeat(32)


def f64(x):
    return np.asarray(x).astype(np.float64)


def striped(idx):
    return np.tile(idx.reshape(-1, 16).T, (8, 1)).astype(np.uint16)


def unstriped(offs):
    return offs[:16].T.reshape(-1).astype(np.int64)


def pack_weight(w):
    k, n = w.shape
    w = f64(np.asarray(w, np.float32).astype(ml_dtypes.bfloat16)).reshape(k // 32, 32, n)
    amax = np.abs(w).max(1)
    byte = np.clip(np.where(amax > 0, np.frexp(amax)[1] - 1 + 127 - 7, 1), 1, 254)
    scaled = (w * np.exp2(127.0 - byte)[:, None, :]).reshape(k, n).astype(np.float32)
    words = np.ascontiguousarray(scaled.reshape(k // 512, 128, 4, n).transpose(0, 1, 3, 2)).astype(ml_dtypes.float8_e4m3fn).view(np.uint8)
    return words, np.ascontiguousarray(byte.astype(np.uint8).reshape(k // 512, 16, n))


def unpack_weight(words, scales):
    g, p, n, _ = words.shape
    vals = np.ascontiguousarray(words).view(ml_dtypes.float8_e4m3fn).astype(np.float64) * np.repeat(np.exp2(scales.astype(np.float64) - 127.0), 8, axis=1)[..., None]
    return vals.transpose(0, 1, 3, 2).reshape(g * 512, n)


K, T, S, N, V, U = 1024, 1024, 512, 128, 256, 512


def setup_inputs():
    n = np.random.standard_normal
    s = mx_kscale(K)[:, None]
    packed_xT = pack_weight(n((K, T)) * s)
    return {
        "x_words": packed_xT[0],
        "x_scales": packed_xT[1],
        "w1": (n((K, N)) / np.sqrt(K) / s).astype(np.float32),
        "bitp": (np.where(np.random.uniform(size=(N, U)) < 0.5, 1.0, -1.0)).astype(np.float32),
        "pm": (np.random.uniform(0.0, 3.0, (N, U))).astype(np.float32),
        "offs": striped(np.random.permutation(T)[:S]),
        "left": striped(np.random.permutation(S)[:V]),
        "right": striped(np.random.permutation(S)[:V]),
        "par": striped(np.random.permutation(np.concatenate([np.arange(V), np.random.randint(0, V, U - V)]))),
    }


def reference(x_words, x_scales, w1, bitp, pm, offs, left, right, par):
    xq = unpack_weight(x_words, x_scales)[:, unstriped(offs)]
    y = mxq(f64(w1), 0, "e4m3").T @ xq
    a = y[:, unstriped(left)]
    d1 = y[:, unstriped(right)]
    f = 0.5 * (np.abs(a + d1) - np.abs(a - d1))
    return f64(pm) + np.log(np.exp(-1.0 * (f64(bitp) * f[:, unstriped(par)])) + 1.0)

@@ -1,0 +1,166 @@
+from contextlib import ExitStack
+
+import concourse.mybir as mybir
+
+F32 = mybir.dt.float32
+BF16 = mybir.dt.bfloat16
+I32 = mybir.dt.int32
+U32 = mybir.dt.uint32
+U16 = mybir.dt.uint16
+U8 = mybir.dt.uint8
+FP8X4 = mybir.dt.float8_e4m3fn_x4
+ALU = mybir.AluOpType
+ACT = mybir.ActivationFunctionType
+
+K, T, S, M, V, U = 1024, 1024, 512, 128, 256, 512
+FLOPS = 2 * K * S * M
+
+P = 128
+PACK = 4
+K_PASS = P * PACK
+PASSES = K // K_PASS
+STRIPE = 16
+QUADRANT = 32
+SCALE_ROWS = 4
+PIECES = ((0, 256), (256, 384), (384, 512))
+HALVES = ((0, 256), (256, 512))
+
+
+def entries(offsets, lo, hi):
+    return offsets[:, lo // STRIPE : hi // STRIPE]
+
+
+def tile_picked_ypolar_metric_p_kernel(
+    tc, x_words, x_scales, w1, bitp, pm, offs, left, right, par, out
+):
+    nc = tc.nc
+    with ExitStack() as ctx:
+        sb = ctx.enter_context(tc.tile_pool(name="sb", bufs=1))
+        ps = ctx.enter_context(tc.psum_pool(name="ps", bufs=1))
+
+        offs_sb = sb.tile([P, S // STRIPE], U16, name="offs_sb")
+        left_sb = sb.tile([P, V // STRIPE], U16, name="left_sb")
+        right_sb = sb.tile([P, V // STRIPE], U16, name="right_sb")
+        par_sb = sb.tile([P, U // STRIPE], U16, name="par_sb")
+
+        word_table = [sb.tile([P, T], U32, name=f"word_table{o}") for o in range(PASSES)]
+        scale_table = sb.tile([P, T], U8, name="scale_table")
+        w_raw = [sb.tile([P, PACK, M], F32, name=f"w_raw{o}") for o in range(PASSES)]
+        bit_sb = sb.tile([P, U], F32, name="bit_sb")
+        pm_sb = sb.tile([P, U], F32, name="pm_sb")
+
+        def load_words(o):
+            nc.sync.dma_start(
+                out=word_table[o][:].bitcast(I32),
+                in_=x_words[o].rearrange("p c r -> p (c r)").bitcast(I32),
+            )
+
+        nc.vector.memset(scale_table[:].bitcast(I32), 0)
+        load_words(0)
+        nc.sync.dma_start(offs_sb[:], offs)
+        for q in range(P // QUADRANT):
+            nc.sync.dma_start(
+                out=scale_table[QUADRANT * q : QUADRANT * q + PASSES * SCALE_ROWS, :].bitcast(I32),
+                in_=x_scales[:, SCALE_ROWS * q : SCALE_ROWS * (q + 1), :].bitcast(I32),
+            )
+        for o in range(PASSES):
+            nc.sync.dma_start(
+                out=w_raw[o][:],
+                in_=w1[K_PASS * o : K_PASS * (o + 1), :].rearrange("(p j) m -> p j m", j=PACK),
+            )
+        load_words(1)
+        nc.sync.dma_start(left_sb[:], left)
+        nc.sync.dma_start(right_sb[:], right)
+        nc.sync.dma_start(par_sb[:], par)
+        nc.sync.dma_start(out=bit_sb[:], in_=bitp)
+        nc.sync.dma_start(out=pm_sb[:], in_=pm)
+
+        x_codes0 = sb.tile([P, S], U32, name="x_codes0", align_bytes=64)
+        nc.vector.tensor_copy(x_codes0[:], word_table[0][:].indirect(offs_sb[:]))
+        x_bytes = sb.tile([P, S], U8, name="x_bytes", align_bytes=64)
+        nc.vector.tensor_copy(x_bytes[:], scale_table[:].indirect(offs_sb[:]))
+
+        w_codes, w_bytes = [], []
+        w_bf = sb.tile([P, PASSES, M, PACK], BF16, name="w_bf", tag="stage", align_bytes=64)
+        for o in range(PASSES):
+            nc.scalar.activation(
+                out=w_bf[:, o].rearrange("p (c i) t -> p c t i", i=4),
+                in_=w_raw[o][:].rearrange("p t (c i) -> p c t i", i=4),
+                func=ACT.Copy,
+            )
+            codes = sb.tile([P, M], U32, name=f"w_codes{o}", align_bytes=64)
+            scales = sb.tile([P, M], U8, name=f"w_bytes{o}", align_bytes=64)
+            nc.vector.quantize_mx(
+                out=codes[:].bitcast(FP8X4),
+                scales=scales[:],
+                in_=w_bf[:, o].rearrange("p m t -> p (m t)"),
+            )
+            w_codes.append(codes)
+            w_bytes.append(scales)
+
+        banks = [ps.tile([P, hi - lo], F32, name=f"bank{lo}") for lo, hi in PIECES]
+        for bank, (lo, hi) in zip(banks, PIECES):
+            nc.tensor.matmul_mx(
+                out=bank[:],
+                lhsT=w_codes[0][:].bitcast(FP8X4),
+                lhsT_scale=w_bytes[0][:],
+                rhs=x_codes0[:, lo:hi].bitcast(FP8X4),
+                rhs_scale=x_bytes[:, lo:hi],
+                start=True,
+                stop=False,
+            )
+
+        y = sb.tile([P, S], F32, name="y")
+        x_codes1 = sb.tile([P, S], U32, name="x_codes1", tag="stage", align_bytes=64)
+        for bank, (lo, hi) in zip(banks, PIECES):
+            nc.vector.tensor_copy(x_codes1[:, lo:hi], word_table[1][:].indirect(entries(offs_sb, lo, hi)))
+            nc.tensor.matmul_mx(
+                out=bank[:],
+                lhsT=w_codes[1][:].bitcast(FP8X4),
+                lhsT_scale=w_bytes[1][:],
+                rhs=x_codes1[:, lo:hi].bitcast(FP8X4),
+                rhs_scale=x_bytes[SCALE_ROWS:, lo:hi],
+                start=False,
+                stop=True,
+            )
+            if hi < S:
+                nc.scalar.copy(out=y[:, lo:hi], in_=bank[:])
+            else:
+                nc.vector.tensor_copy(out=y[:, lo:hi], in_=bank[:])
+
+        pair = sb.tile([P, 2 * V], F32, name="pair")
+        a, d = pair[:, :V], pair[:, V:]
+        nc.vector.tensor_copy(a, y[:].indirect(left_sb[:]))
+        nc.scalar.activation(out=d, in_=y[:].indirect(right_sb[:]), func=ACT.Copy)
+
+        size = sb.tile([P, 2 * V], F32, name="size")
+        nc.scalar.activation(out=size[:], in_=pair[:], func=ACT.Abs)
+        decay = sb.tile([P, 2 * V], F32, name="decay")
+        nc.scalar.activation(out=decay[:], in_=size[:], func=ACT.Exp, scale=-1.0)
+
+        check = sb.tile([P, 2 * V], F32, name="check")
+        soft = sb.tile([P, 2 * V], F32, name="soft")
+        neg_f, low = check[:, :V], check[:, V:]
+        log_term, high = soft[:, :V], soft[:, V:]
+        nc.vector.tensor_tensor(low, a, d, ALU.min)
+        nc.vector.tensor_tensor(high, a, d, ALU.max)
+        nc.vector.scalar_tensor_tensor(neg_f, low, -1.0, high, ALU.mult, ALU.min)
+
+        decay_f = sb.tile([P, V], F32, name="decay_f")
+        nc.vector.tensor_tensor(decay_f[:], decay[:, :V], decay[:, V:], ALU.max)
+        nc.scalar.activation(out=log_term, in_=decay_f[:], func=ACT.Ln, bias=1.0)
+
+        z = sb.tile([P, U], F32, name="z")
+        base = sb.tile([P, U], F32, name="base")
+        result = sb.tile([P, U], F32, name="result")
+        for lo, hi in HALVES:
+            nc.vector.tensor_tensor(
+                z[:, lo:hi], check[:].indirect(entries(par_sb, lo, hi)), bit_sb[:, lo:hi], ALU.mult
+            )
+        for lo, hi in HALVES:
+            nc.vector.scalar_tensor_tensor(base[:, lo:hi], z[:, lo:hi], 0.0, pm_sb[:, lo:hi], ALU.max, ALU.add)
+        for lo, hi in HALVES:
+            nc.vector.tensor_tensor(
+                result[:, lo:hi], soft[:].indirect(entries(par_sb, lo, hi)), base[:, lo:hi], ALU.add
+            )
+            nc.sync.dma_start(out=out[:, lo:hi], in_=result[:, lo:hi])

@@ -45,7 +45,7 @@ def tile_picked_ypolar_metric_p_kernel(
 
         word_table = [sb.tile([P, T], U32, name=f"word_table{o}") for o in range(PASSES)]
         scale_table = sb.tile([P, T], U8, name="scale_table")
-        w_raw = [sb.tile([P, PACK, M], F32, name=f"w_raw{o}") for o in range(PASSES)]
+        w_raw = [sb.tile([P, PACK, M], F32, name=f"w_raw{o}", tag=f"stage{o}", align_bytes=64) for o in range(PASSES)]
         bit_sb = sb.tile([P, U], F32, name="bit_sb")
         pm_sb = sb.tile([P, U], F32, name="pm_sb")
 
@@ -81,10 +81,10 @@ def tile_picked_ypolar_metric_p_kernel(
         nc.vector.tensor_copy(x_bytes[:], scale_table[:].indirect(offs_sb[:]))
 
         w_codes, w_bytes = [], []
-        w_bf = sb.tile([P, PASSES, M, PACK], BF16, name="w_bf", tag="stage", align_bytes=64)
         for o in range(PASSES):
+            w_bf = sb.tile([P, M, PACK], BF16, name=f"w_bf{o}", align_bytes=64)
             nc.scalar.activation(
-                out=w_bf[:, o].rearrange("p (c i) t -> p c t i", i=4),
+                out=w_bf[:].rearrange("p (c i) t -> p c t i", i=4),
                 in_=w_raw[o][:].rearrange("p t (c i) -> p c t i", i=4),
                 func=ACT.Copy,
             )
@@ -93,7 +93,7 @@ def tile_picked_ypolar_metric_p_kernel(
             nc.vector.quantize_mx(
                 out=codes[:].bitcast(FP8X4),
                 scales=scales[:],
-                in_=w_bf[:, o].rearrange("p m t -> p (m t)"),
+                in_=w_bf[:].rearrange("p m t -> p (m t)"),
             )
             w_codes.append(codes)
             w_bytes.append(scales)
@@ -111,7 +111,7 @@ def tile_picked_ypolar_metric_p_kernel(
             )
 
         y = sb.tile([P, S], F32, name="y")
-        x_codes1 = sb.tile([P, S], U32, name="x_codes1", tag="stage", align_bytes=64)
+        x_codes1 = sb.tile([P, S], U32, name="x_codes1", tag="stage1", align_bytes=64)
         for bank, (lo, hi) in zip(banks, PIECES):
             nc.vector.tensor_copy(x_codes1[:, lo:hi], word_table[1][:].indirect(entries(offs_sb, lo, hi)))
             nc.tensor.matmul_mx(
@@ -128,39 +128,53 @@ def tile_picked_ypolar_metric_p_kernel(
             else:
                 nc.vector.tensor_copy(out=y[:, lo:hi], in_=bank[:])
 
-        pair = sb.tile([P, 2 * V], F32, name="pair")
-        a, d = pair[:, :V], pair[:, V:]
-        nc.vector.tensor_copy(a, y[:].indirect(left_sb[:]))
-        nc.scalar.activation(out=d, in_=y[:].indirect(right_sb[:]), func=ACT.Copy)
+        half = V // 2
+        pair = [sb.tile([P, 2, half], F32, name=f"pair{h}") for h in range(2)]
+        for h in range(2):
+            lo, hi = h * half, (h + 1) * half
+            nc.vector.tensor_copy(pair[h][:, 0, :], y[:].indirect(entries(left_sb, lo, hi)))
+            nc.scalar.activation(out=pair[h][:, 1, :], in_=y[:].indirect(entries(right_sb, lo, hi)), func=ACT.Copy)
 
-        size = sb.tile([P, 2 * V], F32, name="size")
-        nc.scalar.activation(out=size[:], in_=pair[:], func=ACT.Abs)
-        decay = sb.tile([P, 2 * V], F32, name="decay")
-        nc.scalar.activation(out=decay[:], in_=size[:], func=ACT.Exp, scale=-1.0)
+        size = [sb.tile([P, 2, half], F32, name=f"size{h}") for h in range(2)]
+        decay = [sb.tile([P, 2, half], F32, name=f"decay{h}") for h in range(2)]
+        for h in range(2):
+            nc.scalar.activation(out=size[h][:], in_=pair[h][:], func=ACT.Abs)
+        for h in range(2):
+            nc.scalar.activation(out=decay[h][:], in_=size[h][:], func=ACT.Exp, scale=-1.0)
 
         check = sb.tile([P, 2 * V], F32, name="check")
         soft = sb.tile([P, 2 * V], F32, name="soft")
         neg_f, low = check[:, :V], check[:, V:]
         log_term, high = soft[:, :V], soft[:, V:]
-        nc.vector.tensor_tensor(low, a, d, ALU.min)
-        nc.vector.tensor_tensor(high, a, d, ALU.max)
-        nc.vector.scalar_tensor_tensor(neg_f, low, -1.0, high, ALU.mult, ALU.min)
-
-        decay_f = sb.tile([P, V], F32, name="decay_f")
-        nc.vector.tensor_tensor(decay_f[:], decay[:, :V], decay[:, V:], ALU.max)
-        nc.scalar.activation(out=log_term, in_=decay_f[:], func=ACT.Ln, bias=1.0)
+        for h in range(2):
+            cols = slice(h * half, (h + 1) * half)
+            nc.vector.tensor_tensor(low[:, cols], pair[h][:, 0, :], pair[h][:, 1, :], ALU.min)
+            nc.vector.tensor_tensor(high[:, cols], pair[h][:, 0, :], pair[h][:, 1, :], ALU.max)
+        for h in range(2):
+            cols = slice(h * half, (h + 1) * half)
+            nc.vector.scalar_tensor_tensor(neg_f[:, cols], low[:, cols], -1.0, high[:, cols], ALU.mult, ALU.min)
 
         z = sb.tile([P, U], F32, name="z")
         base = sb.tile([P, U], F32, name="base")
         result = sb.tile([P, U], F32, name="result")
-        for lo, hi in HALVES:
+        def signed_check(lo, hi):
             nc.vector.tensor_tensor(
                 z[:, lo:hi], check[:].indirect(entries(par_sb, lo, hi)), bit_sb[:, lo:hi], ALU.mult
             )
+
+        signed_check(*HALVES[0])
+        decay_f = sb.tile([P, V], F32, name="decay_f")
+        for h in range(2):
+            cols = slice(h * half, (h + 1) * half)
+            nc.vector.tensor_tensor(decay_f[:, cols], decay[h][:, 0, :], decay[h][:, 1, :], ALU.max)
+        nc.scalar.activation(out=log_term, in_=decay_f[:], func=ACT.Ln, bias=1.0)
+        signed_check(*HALVES[1])
         for lo, hi in HALVES:
             nc.vector.scalar_tensor_tensor(base[:, lo:hi], z[:, lo:hi], 0.0, pm_sb[:, lo:hi], ALU.max, ALU.add)
-        for lo, hi in HALVES:
-            nc.vector.tensor_tensor(
-                result[:, lo:hi], soft[:].indirect(entries(par_sb, lo, hi)), base[:, lo:hi], ALU.add
-            )
-            nc.sync.dma_start(out=out[:, lo:hi], in_=result[:, lo:hi])
+        cut = 256
+        nc.vector.tensor_tensor(result[:, :cut], soft[:].indirect(entries(par_sb, 0, cut)), base[:, :cut], ALU.add)
+        nc.sync.dma_start(out=out[:, :cut], in_=result[:, :cut])
+        fetched = sb.tile([P, U - cut], F32, name="fetched")
+        nc.scalar.activation(out=fetched[:], in_=soft[:].indirect(entries(par_sb, cut, U)), func=ACT.Copy)
+        nc.vector.tensor_tensor(result[:, cut:], fetched[:], base[:, cut:], ALU.add)
+        nc.sync.dma_start(out=out[:, cut:], in_=result[:, cut:])

from contextlib import ExitStack

import concourse.mybir as mybir

F32 = mybir.dt.float32
BF16 = mybir.dt.bfloat16
I32 = mybir.dt.int32
U32 = mybir.dt.uint32
U16 = mybir.dt.uint16
U8 = mybir.dt.uint8
FP8X4 = mybir.dt.float8_e4m3fn_x4
ALU = mybir.AluOpType
ACT = mybir.ActivationFunctionType

K, T, S, M, V, U = 1024, 1024, 512, 128, 256, 512
FLOPS = 2 * K * S * M

P = 128
PACK = 4
K_PASS = P * PACK
PASSES = K // K_PASS
STRIPE = 16
QUADRANT = 32
SCALE_ROWS = 4
PIECES = ((0, 256), (256, 384), (384, 512))
HALVES = ((0, 256), (256, 512))


def entries(offsets, lo, hi):
    return offsets[:, lo // STRIPE : hi // STRIPE]


def tile_picked_ypolar_metric_p_kernel(
    tc, x_words, x_scales, w1, bitp, pm, offs, left, right, par, out
):
    nc = tc.nc
    with ExitStack() as ctx:
        sb = ctx.enter_context(tc.tile_pool(name="sb", bufs=1))
        ps = ctx.enter_context(tc.psum_pool(name="ps", bufs=1))

        offs_sb = sb.tile([P, S // STRIPE], U16, name="offs_sb")
        left_sb = sb.tile([P, V // STRIPE], U16, name="left_sb")
        right_sb = sb.tile([P, V // STRIPE], U16, name="right_sb")
        par_sb = sb.tile([P, U // STRIPE], U16, name="par_sb")

        word_table = [sb.tile([P, T], U32, name=f"word_table{o}") for o in range(PASSES)]
        scale_table = sb.tile([P, T], U8, name="scale_table")
        w_raw = [sb.tile([P, PACK, M], F32, name=f"w_raw{o}", tag=f"stage{o}", align_bytes=64) for o in range(PASSES)]
        bit_sb = sb.tile([P, U], F32, name="bit_sb")
        pm_sb = sb.tile([P, U], F32, name="pm_sb")

        def load_words(o):
            nc.sync.dma_start(
                out=word_table[o][:].bitcast(I32),
                in_=x_words[o].rearrange("p c r -> p (c r)").bitcast(I32),
            )

        nc.vector.memset(scale_table[:].bitcast(I32), 0)
        load_words(0)
        nc.sync.dma_start(offs_sb[:], offs)
        for q in range(P // QUADRANT):
            nc.sync.dma_start(
                out=scale_table[QUADRANT * q : QUADRANT * q + PASSES * SCALE_ROWS, :].bitcast(I32),
                in_=x_scales[:, SCALE_ROWS * q : SCALE_ROWS * (q + 1), :].bitcast(I32),
            )
        for o in range(PASSES):
            nc.sync.dma_start(
                out=w_raw[o][:],
                in_=w1[K_PASS * o : K_PASS * (o + 1), :].rearrange("(p j) m -> p j m", j=PACK),
            )
        load_words(1)
        nc.sync.dma_start(left_sb[:], left)
        nc.sync.dma_start(right_sb[:], right)
        nc.sync.dma_start(par_sb[:], par)
        nc.sync.dma_start(out=bit_sb[:], in_=bitp)
        nc.sync.dma_start(out=pm_sb[:], in_=pm)

        x_codes0 = sb.tile([P, S], U32, name="x_codes0", align_bytes=64)
        nc.vector.tensor_copy(x_codes0[:], word_table[0][:].indirect(offs_sb[:]))
        x_bytes = sb.tile([P, S], U8, name="x_bytes", align_bytes=64)
        nc.vector.tensor_copy(x_bytes[:], scale_table[:].indirect(offs_sb[:]))

        w_codes, w_bytes = [], []
        for o in range(PASSES):
            w_bf = sb.tile([P, M, PACK], BF16, name=f"w_bf{o}", align_bytes=64)
            nc.scalar.activation(
                out=w_bf[:].rearrange("p (c i) t -> p c t i", i=4),
                in_=w_raw[o][:].rearrange("p t (c i) -> p c t i", i=4),
                func=ACT.Copy,
            )
            codes = sb.tile([P, M], U32, name=f"w_codes{o}", align_bytes=64)
            scales = sb.tile([P, M], U8, name=f"w_bytes{o}", align_bytes=64)
            nc.vector.quantize_mx(
                out=codes[:].bitcast(FP8X4),
                scales=scales[:],
                in_=w_bf[:].rearrange("p m t -> p (m t)"),
            )
            w_codes.append(codes)
            w_bytes.append(scales)

        banks = [ps.tile([P, hi - lo], F32, name=f"bank{lo}") for lo, hi in PIECES]
        for bank, (lo, hi) in zip(banks, PIECES):
            nc.tensor.matmul_mx(
                out=bank[:],
                lhsT=w_codes[0][:].bitcast(FP8X4),
                lhsT_scale=w_bytes[0][:],
                rhs=x_codes0[:, lo:hi].bitcast(FP8X4),
                rhs_scale=x_bytes[:, lo:hi],
                start=True,
                stop=False,
            )

        y = sb.tile([P, S], F32, name="y")
        x_codes1 = sb.tile([P, S], U32, name="x_codes1", tag="stage1", align_bytes=64)
        for bank, (lo, hi) in zip(banks, PIECES):
            nc.vector.tensor_copy(x_codes1[:, lo:hi], word_table[1][:].indirect(entries(offs_sb, lo, hi)))
            nc.tensor.matmul_mx(
                out=bank[:],
                lhsT=w_codes[1][:].bitcast(FP8X4),
                lhsT_scale=w_bytes[1][:],
                rhs=x_codes1[:, lo:hi].bitcast(FP8X4),
                rhs_scale=x_bytes[SCALE_ROWS:, lo:hi],
                start=False,
                stop=True,
            )
            if hi < S:
                nc.scalar.copy(out=y[:, lo:hi], in_=bank[:])
            else:
                nc.vector.tensor_copy(out=y[:, lo:hi], in_=bank[:])

        half = V // 2
        pair = [sb.tile([P, 2, half], F32, name=f"pair{h}") for h in range(2)]
        for h in range(2):
            lo, hi = h * half, (h + 1) * half
            nc.vector.tensor_copy(pair[h][:, 0, :], y[:].indirect(entries(left_sb, lo, hi)))
            nc.scalar.activation(out=pair[h][:, 1, :], in_=y[:].indirect(entries(right_sb, lo, hi)), func=ACT.Copy)

        size = [sb.tile([P, 2, half], F32, name=f"size{h}") for h in range(2)]
        decay = [sb.tile([P, 2, half], F32, name=f"decay{h}") for h in range(2)]
        for h in range(2):
            nc.scalar.activation(out=size[h][:], in_=pair[h][:], func=ACT.Abs)
        for h in range(2):
            nc.scalar.activation(out=decay[h][:], in_=size[h][:], func=ACT.Exp, scale=-1.0)

        check = sb.tile([P, 2 * V], F32, name="check")
        soft = sb.tile([P, 2 * V], F32, name="soft")
        neg_f, low = check[:, :V], check[:, V:]
        log_term, high = soft[:, :V], soft[:, V:]
        for h in range(2):
            cols = slice(h * half, (h + 1) * half)
            nc.vector.tensor_tensor(low[:, cols], pair[h][:, 0, :], pair[h][:, 1, :], ALU.min)
            nc.vector.tensor_tensor(high[:, cols], pair[h][:, 0, :], pair[h][:, 1, :], ALU.max)
        for h in range(2):
            cols = slice(h * half, (h + 1) * half)
            nc.vector.scalar_tensor_tensor(neg_f[:, cols], low[:, cols], -1.0, high[:, cols], ALU.mult, ALU.min)

        z = sb.tile([P, U], F32, name="z")
        base = sb.tile([P, U], F32, name="base")
        result = sb.tile([P, U], F32, name="result")
        def signed_check(lo, hi):
            nc.vector.tensor_tensor(
                z[:, lo:hi], check[:].indirect(entries(par_sb, lo, hi)), bit_sb[:, lo:hi], ALU.mult
            )

        signed_check(*HALVES[0])
        decay_f = sb.tile([P, V], F32, name="decay_f")
        for h in range(2):
            cols = slice(h * half, (h + 1) * half)
            nc.vector.tensor_tensor(decay_f[:, cols], decay[h][:, 0, :], decay[h][:, 1, :], ALU.max)
        nc.scalar.activation(out=log_term, in_=decay_f[:], func=ACT.Ln, bias=1.0)
        signed_check(*HALVES[1])
        for lo, hi in HALVES:
            nc.vector.scalar_tensor_tensor(base[:, lo:hi], z[:, lo:hi], 0.0, pm_sb[:, lo:hi], ALU.max, ALU.add)
        cut = 256
        nc.vector.tensor_tensor(result[:, :cut], soft[:].indirect(entries(par_sb, 0, cut)), base[:, :cut], ALU.add)
        nc.sync.dma_start(out=out[:, :cut], in_=result[:, :cut])
        fetched = sb.tile([P, U - cut], F32, name="fetched")
        nc.scalar.activation(out=fetched[:], in_=soft[:].indirect(entries(par_sb, cut, U)), func=ACT.Copy)
        nc.vector.tensor_tensor(result[:, cut:], fetched[:], base[:, cut:], ALU.add)
        nc.sync.dma_start(out=out[:, cut:], in_=result[:, cut:])
